import numpy as np
CORES = [16,17,18,19,20,21,22,23,184,185,186,187,188,189,190,191]
N = 16
ROUNDS = 4
def setup_inputs(rng):
    return {"x": rng.standard_normal((N, ROUNDS, 128, 256), dtype=np.float32)}
def reference(x):
    b = 256 // N
    blocks = x.reshape(N, ROUNDS, 128, N, b)
    return {"y": np.ascontiguousarray(blocks.transpose(3, 1, 2, 0, 4)).reshape(N, ROUNDS, 128, 256)}

import concourse.bass as bass

ROUNDS = 4
N = 16
B = 256 // N
HALF = 128
GATEWAYS = (2, 3, 6, 7)

SCRATCH = {
    "z": ("sbuf", [128, 768], "float32"),
}
SEMAPHORES = ["loc", "sent", "arr0", "arr1", "aux0", "aux1"]


def is_gateway(rank):
    return rank % 8 in GATEWAYS


def send_base(rank, k):
    return 256 * (k % 2) if is_gateway(rank) else 256 * ((k + 1) % 3)


def land_base(rank, k):
    return 256 * ((k + 1) % 2) if is_gateway(rank) else 256 * (k % 3)


def pass_base(k):
    return 512 + HALF * (k % 2)


def rank_program(g, core, T, topo):
    me = T.rank_of(core)
    if me is None:
        return
    z = T.z
    sem = T.sem
    aux = (sem.aux0, sem.aux1)
    chip = me // 8
    near = [r for r in range(8 * chip, 8 * chip + 8) if r != me]
    far = list(range(8 * (1 - chip), 8 * (1 - chip) + 8))
    count = {"loc": 0, "sent": 0}

    def arrival_sem(rank, k):
        if is_gateway(rank):
            return (sem.arr0, sem.arr1)[k % 2]
        return (sem.arr0, sem.arr1, sem.aux0, sem.aux1)[k]

    def local(out, in_):
        g.dma_start(out, in_).then_inc(sem.loc, 16)
        count["loc"] += 16

    def wait_local():
        g.wait_ge(sem.loc, count["loc"])

    def wait_sent():
        g.wait_ge(sem.sent, count["sent"])

    def load(k):
        s = send_base(me, k)
        local(z[:, s:s + 256], T.x[k])

    def store(k):
        s = land_base(me, k)
        local(T.y[k], z[:, s:s + 256])

    def wait_round(k):
        g.wait_ge(arrival_sem(me, k), 15 * (k // 2 + 1) if is_gateway(me) else 15)

    def block(k, src_col, origin, dst, engine):
        rid, pid = topo.addr(T.cores[dst], core)
        d = land_base(dst, k) + B * origin
        return bass.RemoteDMATransfer(dst_ids=[bass.DstId(rid=rid, pnc=pid)], dma_engine_mask=1 << engine,
                                      remote_sem=arrival_sem(dst, k), src=z[:, src_col:src_col + B], dst=z[:, d:d + B])

    def fused(transfers):
        g.remote_dma_fused(transfers, local_sem=sem.sent)
        count["sent"] += len(transfers)

    def own(k, dsts, first_engine):
        s = send_base(me, k)
        return [block(k, s + B * d, me, d, first_engine + i) for i, d in enumerate(dsts)]

    def own_block_of_round_0():
        d = land_base(me, 0) + B * me
        local(z[:, d:d + B], T.x[0, :, B * me:B * (me + 1)])

    def finish():
        wait_local()
        local(T.y[1:ROUNDS, :, B * me:B * (me + 1)], T.x[1:ROUNDS, :, B * me:B * (me + 1)])
        wait_local()
        wait_sent()

    if not is_gateway(me):
        gate = me + 2
        rid, pid = topo.addr(T.cores[gate], core)

        def hand_over(k):
            s = send_base(me, k) + HALF * (1 - chip)
            f = pass_base(k)
            g.remote_dma(z[:, f:f + HALF], z[:, s:s + HALF], aux[k % 2], sem.sent, pid, rid, 0xFFFF)
            count["sent"] += 16

        load(0)
        load(1)
        own_block_of_round_0()
        wait_local()
        hand_over(0)
        hand_over(1)
        fused(own(0, near, 0))
        for k in range(1, ROUNDS):
            wait_round(k - 1)
            fused(own(k, near, 0))
            store(k - 1)
            if k + 1 < ROUNDS:
                wait_local()
                load(k + 1)
                wait_local()
                hand_over(k + 1)
        wait_round(ROUNDS - 1)
        store(ROUNDS - 1)
        finish()
        return

    mate = me - 2
    far_partners = [d for d in far if not is_gateway(d)]
    far_gateways = [d for d in far if is_gateway(d)]

    def passed(k, dsts, first_engine):
        f = pass_base(k)
        return [block(k, f + B * (d % 8), mate, d, first_engine + i) for i, d in enumerate(dsts)]

    own_block_of_round_0()
    for k in range(ROUNDS):
        if k > 0:
            wait_round(k - 1)
            store(k - 1)
            wait_local()
        load(k)
        wait_local()
        g.wait_ge(aux[k % 2], 16 * (k // 2 + 1))
        frees_f = k + 2 < ROUNDS
        first_near = [d for d in near if d != mate] if frees_f else near
        fused(own(k, far_partners, 0) + passed(k, far_partners, 4) + own(k, first_near, 8))
        if k + 1 < ROUNDS:
            wait_sent()
        fused(own(k, far_gateways, 0) + passed(k, far_gateways, 4))
        if frees_f:
            wait_sent()
            fused(own(k, [mate], 8))
    wait_round(ROUNDS - 1)
    store(ROUNDS - 1)
    finish()
